import numpy as np, ml_dtypes
CORES = [35,38,43,46]
N = 4
import mx_ref
NC, G = 256, 4
C = np.float32(0.029)
BF = ml_dtypes.bfloat16
def cut(t, i, w=512):
    return t[:, w * i:w * i + w]
def tile(rs):
    return np.stack(rs, axis=2).reshape(128, -1).astype(BF)
def layer(w, X):
    out = []
    for i in range(G):
        for t in range(len(X)):
            p = mx_ref.matmul(mx_ref.quantize(cut(w, len(X) * i + t)), X[t])
            z = p if t == 0 else z + p
        out.append(z)
    return out
def masked(A, E):
    return [(e * (a > 0)) * C for a, e in zip(A, E)]
def setup_inputs(rng):
    def f(*shape):
        return mx_ref.flush((rng.standard_normal(shape, dtype=np.float32) * np.exp2(rng.integers(-2, 3, shape[:-1] + (1,)))).astype(BF))
    return {"x": f(N, 128, 512), "e": f(N, 128, 512), "a": f(N, 128, G * 512), "v": f(N, 128, 4 * NC)}
def setup_inputs_blocks(rng):
    d = setup_inputs(rng)
    for k in ("x", "e", "a", "v"): d[k] = mx_ref.spread(d[k], rng, 4)
    return d
def setup_inputs_wide(rng):
    d = setup_inputs(rng)
    for k in ("x", "e", "a", "v"): d[k] = mx_ref.flush((d[k].astype(np.float32) * np.exp2(rng.integers(-6, 7, (N, 1, 1))).astype(np.float32)).astype(BF))
    return d
def setup_inputs_zeros(rng):
    d = setup_inputs(rng); v = d["x"].reshape(N, 128, -1, 4).copy()
    v[np.broadcast_to((rng.random((N, 1, v.shape[2], 1)) < 0.33), v.shape)] = 0
    d["x"] = v.reshape(d["x"].shape)
    return d
def reference(x, e, a, v):
    T = [mx_ref.quantize(tile(masked(layer(a[j], [mx_ref.quantize(x[j])]), layer(a[j], [mx_ref.quantize(e[j])])))) for j in range(N)]
    y = np.zeros((N, 128, N * NC), np.float32)
    for r in range(N):
        qv = mx_ref.quantize(v[r])
        for j in range(N):
            y[r][:, NC * j:NC * j + NC] = mx_ref.matmul(T[j], qv)
    return {"y": y}

@@ -1,0 +1,149 @@
+from concourse.bass import DstId, RemoteDMATransfer
+from concourse.mybir import dt, AluOpType, ActivationFunctionType
+
+N = 4
+G = 4
+W = 128
+NV = 256
+BANK = 512
+CONST = 0.029
+
+SCRATCH = {
+    "xe_t": ("sbuf", [128, 8 * W], "bfloat16"),
+    "a_t": ("sbuf", [128, 4 * G * W], "bfloat16"),
+    "v_t": ("sbuf", [128, 4 * NV], "bfloat16"),
+    "xe_q": ("sbuf", [128, 2 * W], "float8_e4m3fn_x4"),
+    "xe_s": ("sbuf", [128, 2 * W], "uint8"),
+    "a_q": ("sbuf", [128, G * W], "float8_e4m3fn_x4"),
+    "a_s": ("sbuf", [128, G * W], "uint8"),
+    "v_q": ("sbuf", [128, NV], "float8_e4m3fn_x4"),
+    "v_s": ("sbuf", [128, NV], "uint8"),
+    "mc": ("sbuf", [128, G * W], "float32"),
+    "t_t": ("sbuf", [128, 4 * W], "bfloat16"),
+    "t_q": ("sbuf", [128, N * W], "float8_e4m3fn_x4"),
+    "t_s": ("sbuf", [128, N * W], "uint8"),
+    "y_t": ("sbuf", [128, N * NV], "float32"),
+    "ps1": ("psum", [128, G * BANK], "float32"),
+    "ps2": ("psum", [128, N * BANK], "float32"),
+}
+SEMAPHORES = (["ld_xe", "ld_a0", "ld_a1", "ld_v", "q_xe", "q_t", "q_v", "sent", "st_sy", "st_sc"]
+              + ["q_a%d" % i for i in range(G)] + ["mm%d" % i for i in range(G)]
+              + ["ts%d" % i for i in range(G)] + ["tt%d" % i for i in range(G)]
+              + ["arr%d" % i for i in range(N)] + ["pm%d" % i for i in range(N)] + ["cp%d" % i for i in range(N)])
+
+
+def engines(mask):
+    return sum((mask >> b) & 1 for b in range(mask.bit_length()))
+
+
+def rounds_of(src, cores, topo):
+    others = [c for c in cores if c != src]
+    near = [c for c in others if topo.chip(c) == topo.chip(src)]
+    far = [c for c in others if topo.chip(c) != topo.chip(src)]
+    far.sort(key=lambda c: topo.die(c) != topo.die(src))
+    leave = topo.mask(src, far[0])
+    stay = topo.mask(src, near[0]) & ~leave
+    return [[(far[0], leave)], [(far[1], leave), (near[0], stay)]]
+
+
+def rank_program(g, core, T, topo):
+    r = T.rank_of(core)
+    if r is None:
+        return
+    S = T.sem
+    V, TE, AC, SY = g.vector, g.tensor, g.scalar, g.sync
+
+    def slot(buf, i, w=W):
+        return buf[:, w * i:w * i + w]
+
+    due = {}
+    for j, c in enumerate(T.cores):
+        if c == core:
+            continue
+        for k, rnd in enumerate(rounds_of(c, T.cores, topo)):
+            for dst, m in rnd:
+                if dst == core:
+                    due[j] = (k, topo.chip(c) != topo.chip(core), 2 * engines(m))
+    order = sorted(due, key=lambda j: (due[j][1], due[j][0]))
+    seq = [r] + order
+
+    SY.dma_start(T.xe_t[:, 0:4 * W], T.x[:]).then_inc(S.ld_xe, 16)
+    AC.dma_start(T.xe_t[:, 4 * W:8 * W], T.e[:]).then_inc(S.ld_xe, 16)
+    H = 2 * 4 * W
+    SY.dma_start(T.a_t[:, 0:H], T.a[:, 0:H]).then_inc(S.ld_a0, 16)
+    SY.dma_start(T.a_t[:, H:2 * H], T.a[:, H:2 * H]).then_inc(S.ld_a1, 16)
+    SY.dma_start(T.v_t[:], T.v[:]).then_inc(S.ld_v, 16)
+
+    def quant_a(i):
+        V.quantize_mx(slot(T.a_q, i), slot(T.a_s, i), slot(T.a_t, i, 4 * W)).then_inc(S["q_a%d" % i], 1)
+
+    def mask(i):
+        V.wait_ge(S["mm%d" % i], 1)
+        V.tensor_scalar(slot(T.mc, i), T.ps1[:, BANK * i:BANK * i + W], 0.0, CONST,
+                        AluOpType.is_gt, AluOpType.mult).then_inc(S["ts%d" % i], 1)
+        V.wait_ge(S["ts%d" % i], 1)
+        V.tensor_tensor(T.t_t[:, i:4 * W:4], T.ps1[:, BANK * i + W:BANK * i + 2 * W], slot(T.mc, i),
+                        AluOpType.mult).then_inc(S["tt%d" % i], 1)
+
+    V.wait_ge(S.ld_xe, 32)
+    V.quantize_mx(T.xe_q[:], T.xe_s[:], T.xe_t[:]).then_inc(S.q_xe, 1)
+    V.wait_ge(S.ld_a0, 16)
+    quant_a(0)
+    quant_a(1)
+    mask(0)
+    V.wait_ge(S.ld_a1, 16)
+    quant_a(2)
+    quant_a(3)
+    mask(1)
+    mask(2)
+    mask(3)
+    for i in range(G):
+        V.wait_ge(S["tt%d" % i], 1)
+    V.quantize_mx(slot(T.t_q, r), slot(T.t_s, r), T.t_t[:]).then_inc(S.q_t, 1)
+    V.wait_ge(S.ld_v, 16)
+    V.quantize_mx(T.v_q[:], T.v_s[:], T.v_t[:]).then_inc(S.q_v, 1)
+
+    TE.wait_ge(S.q_xe, 1)
+    for i in range(G):
+        TE.wait_ge(S["q_a%d" % i], 1)
+        TE.matmul_mx(T.ps1[:, BANK * i:BANK * i + 2 * W], slot(T.a_q, i), slot(T.a_s, i),
+                     T.xe_q[:], T.xe_s[:], True, True).then_inc(S["mm%d" % i], 1)
+
+    g.wait_ge(S.q_t, 1)
+    left = 0
+    for rnd in rounds_of(core, T.cores, topo):
+        for ap in (slot(T.t_q, r).bitcast(dt.uint8), slot(T.t_s, r)):
+            trs = []
+            for dst, m in rnd:
+                rid, pid, _ = topo.addr(dst)
+                trs.append(RemoteDMATransfer(dst_ids=[DstId(rid=rid, pnc=pid)], dma_engine_mask=m,
+                                             remote_sem=S["arr%d" % r], src=ap, dst=ap))
+                left += engines(m)
+            g.remote_dma_fused(trs, local_sem=S.sent)
+
+    TE.wait_ge(S.q_t, 1)
+    TE.wait_ge(S.q_v, 1)
+    for j in seq:
+        if j != r:
+            TE.wait_ge(S["arr%d" % j], due[j][2])
+        TE.matmul_mx(T.ps2[:, BANK * j:BANK * j + NV], slot(T.t_q, j), slot(T.t_s, j),
+                     T.v_q[:], T.v_s[:], True, True).then_inc(S["pm%d" % j], 1)
+
+    n_sy = n_sc = 0
+    for k, j in enumerate(seq):
+        src, mid, out = T.ps2[:, BANK * j:BANK * j + NV], slot(T.y_t, j, NV), slot(T.y, j, NV)
+        if k % 2 == 0:
+            AC.wait_ge(S["pm%d" % j], 1)
+            AC.activation(mid, src, ActivationFunctionType.Copy).then_inc(S["cp%d" % j], 1)
+            AC.wait_ge(S["cp%d" % j], 1)
+            AC.dma_start(out, mid).then_inc(S.st_sc, 16)
+            n_sc += 16
+        else:
+            V.wait_ge(S["pm%d" % j], 1)
+            V.tensor_copy(mid, src).then_inc(S["cp%d" % j], 1)
+            SY.wait_ge(S["cp%d" % j], 1)
+            SY.dma_start(out, mid).then_inc(S.st_sy, 16)
+            n_sy += 16
+    AC.wait_ge(S.st_sc, n_sc)
+    SY.wait_ge(S.st_sy, n_sy)
+    g.wait_ge(S.sent, left)

@@ -23,27 +23,27 @@ SCRATCH = {
     "t_q": ("sbuf", [128, N * W], "float8_e4m3fn_x4"),
     "t_s": ("sbuf", [128, N * W], "uint8"),
     "y_t": ("sbuf", [128, N * NV], "float32"),
-    "ps1": ("psum", [128, G * BANK], "float32"),
-    "ps2": ("psum", [128, N * BANK], "float32"),
+    "ps": ("psum", [128, 2 * G * BANK], "float32"),
 }
-SEMAPHORES = (["ld_xe", "ld_a0", "ld_a1", "ld_v", "q_xe", "q_t", "q_v", "sent", "st_sy", "st_sc"]
-              + ["q_a%d" % i for i in range(G)] + ["mm%d" % i for i in range(G)]
+SEMAPHORES = (["ld_x", "ld_e", "ld_a", "ld_v", "q_x", "q_e", "q_t", "q_v", "sent", "st_sy", "st_sc", "pm_b", "cp_b"]
+              + ["q_a%d" % i for i in range(G)] + ["mu%d" % i for i in range(G)] + ["md%d" % i for i in range(G)]
               + ["ts%d" % i for i in range(G)] + ["tt%d" % i for i in range(G)]
-              + ["arr%d" % i for i in range(N)] + ["pm%d" % i for i in range(N)] + ["cp%d" % i for i in range(N)])
+              + ["arc%d" % i for i in range(N)] + ["arp%d" % i for i in range(N)]
+              + ["pm%d" % i for i in range(N)] + ["cp%d" % i for i in range(N)])
 
 
 def engines(mask):
     return sum((mask >> b) & 1 for b in range(mask.bit_length()))
 
 
-def rounds_of(src, cores, topo):
+def plan_of(src, cores, topo):
     others = [c for c in cores if c != src]
     near = [c for c in others if topo.chip(c) == topo.chip(src)]
     far = [c for c in others if topo.chip(c) != topo.chip(src)]
     far.sort(key=lambda c: topo.die(c) != topo.die(src))
     leave = topo.mask(src, far[0])
-    stay = topo.mask(src, near[0]) & ~leave
-    return [[(far[0], leave)], [(far[1], leave), (near[0], stay)]]
+    whole = topo.mask(src, near[0])
+    return near[0], far[0], far[1], leave, whole & ~leave, whole
 
 
 def rank_program(g, core, T, topo):
@@ -56,83 +56,100 @@ def rank_program(g, core, T, topo):
     def slot(buf, i, w=W):
         return buf[:, w * i:w * i + w]
 
-    due = {}
-    for j, c in enumerate(T.cores):
-        if c == core:
-            continue
-        for k, rnd in enumerate(rounds_of(c, T.cores, topo)):
-            for dst, m in rnd:
-                if dst == core:
-                    due[j] = (k, topo.chip(c) != topo.chip(core), 2 * engines(m))
-    order = sorted(due, key=lambda j: (due[j][1], due[j][0]))
-    seq = [r] + order
+    def bank(i, w):
+        return T.ps[:, BANK * i:BANK * i + w]
 
-    SY.dma_start(T.xe_t[:, 0:4 * W], T.x[:]).then_inc(S.ld_xe, 16)
-    AC.dma_start(T.xe_t[:, 4 * W:8 * W], T.e[:]).then_inc(S.ld_xe, 16)
-    H = 2 * 4 * W
-    SY.dma_start(T.a_t[:, 0:H], T.a[:, 0:H]).then_inc(S.ld_a0, 16)
-    SY.dma_start(T.a_t[:, H:2 * H], T.a[:, H:2 * H]).then_inc(S.ld_a1, 16)
+    def codes(i):
+        return slot(T.t_q, i).bitcast(dt.uint8)
+
+    near, far1, far2, leave, stay, whole = plan_of(core, T.cores, topo)
+    jn, j1, j2 = T.rank_of(near), T.rank_of(far1), T.rank_of(far2)
+    due = {jn: (engines(stay), engines(stay)), j1: (engines(leave), engines(leave)), j2: (engines(whole), engines(leave))}
+    seq = [r, jn, j1, j2]
+
+    Q = 4 * W
+    SY.dma_start(T.a_t[:], T.a[:]).then_inc(S.ld_a, 16)
+    AC.dma_start(T.xe_t[:, 0:Q], T.x[:]).then_inc(S.ld_x, 16)
+    AC.dma_start(T.xe_t[:, Q:2 * Q], T.e[:]).then_inc(S.ld_e, 16)
     SY.dma_start(T.v_t[:], T.v[:]).then_inc(S.ld_v, 16)
 
-    def quant_a(i):
-        V.quantize_mx(slot(T.a_q, i), slot(T.a_s, i), slot(T.a_t, i, 4 * W)).then_inc(S["q_a%d" % i], 1)
-
-    def mask(i):
-        V.wait_ge(S["mm%d" % i], 1)
-        V.tensor_scalar(slot(T.mc, i), T.ps1[:, BANK * i:BANK * i + W], 0.0, CONST,
-                        AluOpType.is_gt, AluOpType.mult).then_inc(S["ts%d" % i], 1)
+    V.wait_ge(S.ld_x, 16)
+    V.quantize_mx(slot(T.xe_q, 0), slot(T.xe_s, 0), T.xe_t[:, 0:Q]).then_inc(S.q_x, 1)
+    V.wait_ge(S.ld_a, 16)
+    for i in range(G):
+        V.quantize_mx(slot(T.a_q, i), slot(T.a_s, i), slot(T.a_t, i, Q)).then_inc(S["q_a%d" % i], 1)
+    V.wait_ge(S.ld_e, 16)
+    V.quantize_mx(slot(T.xe_q, 1), slot(T.xe_s, 1), T.xe_t[:, Q:2 * Q]).then_inc(S.q_e, 1)
+    for i in range(G):
+        V.wait_ge(S["mu%d" % i], 1)
+        V.tensor_scalar(slot(T.mc, i), bank(i, W), 0.0, CONST, AluOpType.is_gt, AluOpType.mult).then_inc(S["ts%d" % i], 1)
+    for i in range(G):
         V.wait_ge(S["ts%d" % i], 1)
-        V.tensor_tensor(T.t_t[:, i:4 * W:4], T.ps1[:, BANK * i + W:BANK * i + 2 * W], slot(T.mc, i),
-                        AluOpType.mult).then_inc(S["tt%d" % i], 1)
-
-    V.wait_ge(S.ld_xe, 32)
-    V.quantize_mx(T.xe_q[:], T.xe_s[:], T.xe_t[:]).then_inc(S.q_xe, 1)
-    V.wait_ge(S.ld_a0, 16)
-    quant_a(0)
-    quant_a(1)
-    mask(0)
-    V.wait_ge(S.ld_a1, 16)
-    quant_a(2)
-    quant_a(3)
-    mask(1)
-    mask(2)
-    mask(3)
+        V.wait_ge(S["md%d" % i], 1)
+        V.tensor_tensor(T.t_t[:, i:Q:4], bank(G + i, W), slot(T.mc, i), AluOpType.mult).then_inc(S["tt%d" % i], 1)
     for i in range(G):
         V.wait_ge(S["tt%d" % i], 1)
     V.quantize_mx(slot(T.t_q, r), slot(T.t_s, r), T.t_t[:]).then_inc(S.q_t, 1)
     V.wait_ge(S.ld_v, 16)
     V.quantize_mx(T.v_q[:], T.v_s[:], T.v_t[:]).then_inc(S.q_v, 1)
 
-    TE.wait_ge(S.q_xe, 1)
+    TE.wait_ge(S.q_x, 1)
     for i in range(G):
         TE.wait_ge(S["q_a%d" % i], 1)
-        TE.matmul_mx(T.ps1[:, BANK * i:BANK * i + 2 * W], slot(T.a_q, i), slot(T.a_s, i),
-                     T.xe_q[:], T.xe_s[:], True, True).then_inc(S["mm%d" % i], 1)
+        TE.matmul_mx(bank(i, W), slot(T.a_q, i), slot(T.a_s, i),
+                     slot(T.xe_q, 0), slot(T.xe_s, 0), True, True).then_inc(S["mu%d" % i], 1)
+    TE.wait_ge(S.q_e, 1)
+    for i in range(G):
+        TE.matmul_mx(bank(G + i, W), slot(T.a_q, i), slot(T.a_s, i),
+                     slot(T.xe_q, 1), slot(T.xe_s, 1), True, True).then_inc(S["md%d" % i], 1)
+
+    left = [0]
+
+    def send(ap, sem, where):
+        trs = []
+        for dst, m in where:
+            rid, pid, _ = topo.addr(dst)
+            trs.append(RemoteDMATransfer(dst_ids=[DstId(rid=rid, pnc=pid)], dma_engine_mask=m,
+                                         remote_sem=sem, src=ap, dst=ap))
+            left[0] += engines(m)
+        g.remote_dma_fused(trs, local_sem=S.sent)
 
     g.wait_ge(S.q_t, 1)
-    left = 0
-    for rnd in rounds_of(core, T.cores, topo):
-        for ap in (slot(T.t_q, r).bitcast(dt.uint8), slot(T.t_s, r)):
-            trs = []
-            for dst, m in rnd:
-                rid, pid, _ = topo.addr(dst)
-                trs.append(RemoteDMATransfer(dst_ids=[DstId(rid=rid, pnc=pid)], dma_engine_mask=m,
-                                             remote_sem=S["arr%d" % r], src=ap, dst=ap))
-                left += engines(m)
-            g.remote_dma_fused(trs, local_sem=S.sent)
+    send(codes(r), S["arc%d" % r], [(far1, leave), (near, stay)])
+    send(slot(T.t_s, r), S["arp%d" % r], [(far1, leave), (near, stay)])
+    send(slot(T.t_s, r), S["arp%d" % r], [(far2, leave)])
+    g.wait_ge(S["arc%d" % j1], due[j1][0])
+    send(codes(j1), S["arc%d" % j1], [(near, whole)])
 
     TE.wait_ge(S.q_t, 1)
     TE.wait_ge(S.q_v, 1)
+    HV = NV // 2
     for j in seq:
         if j != r:
-            TE.wait_ge(S["arr%d" % j], due[j][2])
-        TE.matmul_mx(T.ps2[:, BANK * j:BANK * j + NV], slot(T.t_q, j), slot(T.t_s, j),
-                     T.v_q[:], T.v_s[:], True, True).then_inc(S["pm%d" % j], 1)
+            TE.wait_ge(S["arc%d" % j], due[j][0])
+            TE.wait_ge(S["arp%d" % j], due[j][1])
+        if j != seq[-1]:
+            TE.matmul_mx(bank(j, NV), slot(T.t_q, j), slot(T.t_s, j),
+                         T.v_q[:], T.v_s[:], True, True).then_inc(S["pm%d" % j], 1)
+        else:
+            TE.matmul_mx(bank(j, HV), slot(T.t_q, j), slot(T.t_s, j),
+                         T.v_q[:, 0:HV], T.v_s[:, 0:HV], True, True).then_inc(S["pm%d" % j], 1)
+            TE.matmul_mx(bank(N, HV), slot(T.t_q, j), slot(T.t_s, j),
+                         T.v_q[:, HV:NV], T.v_s[:, HV:NV], True, True).then_inc(S.pm_b, 1)
 
     n_sy = n_sc = 0
     for k, j in enumerate(seq):
-        src, mid, out = T.ps2[:, BANK * j:BANK * j + NV], slot(T.y_t, j, NV), slot(T.y, j, NV)
-        if k % 2 == 0:
+        src, mid, out = bank(j, NV), slot(T.y_t, j, NV), slot(T.y, j, NV)
+        if k == len(seq) - 1:
+            V.wait_ge(S["pm%d" % j], 1)
+            V.tensor_copy(T.y_t[:, NV * j:NV * j + HV], bank(j, HV)).then_inc(S["cp%d" % j], 1)
+            V.wait_ge(S.pm_b, 1)
+            V.tensor_copy(T.y_t[:, NV * j + HV:NV * j + NV], bank(N, HV)).then_inc(S.cp_b, 1)
+            SY.wait_ge(S["cp%d" % j], 1)
+            SY.wait_ge(S.cp_b, 1)
+            SY.dma_start(out, mid).then_inc(S.st_sy, 16)
+            n_sy += 16
+        elif k % 2 == 0:
             AC.wait_ge(S["pm%d" % j], 1)
             AC.activation(mid, src, ActivationFunctionType.Copy).then_inc(S["cp%d" % j], 1)
             AC.wait_ge(S["cp%d" % j], 1)
@@ -146,4 +163,4 @@ def rank_program(g, core, T, topo):
             n_sy += 16
     AC.wait_ge(S.st_sc, n_sc)
     SY.wait_ge(S.st_sy, n_sy)
-    g.wait_ge(S.sent, left)
+    g.wait_ge(S.sent, left[0])

from concourse.bass import DstId, RemoteDMATransfer
from concourse.mybir import dt, AluOpType, ActivationFunctionType

N = 4
G = 4
W = 128
NV = 256
BANK = 512
CONST = 0.029

SCRATCH = {
    "xe_t": ("sbuf", [128, 8 * W], "bfloat16"),
    "a_t": ("sbuf", [128, 4 * G * W], "bfloat16"),
    "v_t": ("sbuf", [128, 4 * NV], "bfloat16"),
    "xe_q": ("sbuf", [128, 2 * W], "float8_e4m3fn_x4"),
    "xe_s": ("sbuf", [128, 2 * W], "uint8"),
    "a_q": ("sbuf", [128, G * W], "float8_e4m3fn_x4"),
    "a_s": ("sbuf", [128, G * W], "uint8"),
    "v_q": ("sbuf", [128, NV], "float8_e4m3fn_x4"),
    "v_s": ("sbuf", [128, NV], "uint8"),
    "mc": ("sbuf", [128, G * W], "float32"),
    "t_t": ("sbuf", [128, 4 * W], "bfloat16"),
    "t_q": ("sbuf", [128, N * W], "float8_e4m3fn_x4"),
    "t_s": ("sbuf", [128, N * W], "uint8"),
    "y_t": ("sbuf", [128, N * NV], "float32"),
    "ps": ("psum", [128, 2 * G * BANK], "float32"),
}
SEMAPHORES = (["ld_x", "ld_e", "ld_a", "ld_v", "q_x", "q_e", "q_t", "q_v", "sent", "st_sy", "st_sc", "pm_b", "cp_b"]
              + ["q_a%d" % i for i in range(G)] + ["mu%d" % i for i in range(G)] + ["md%d" % i for i in range(G)]
              + ["ts%d" % i for i in range(G)] + ["tt%d" % i for i in range(G)]
              + ["arc%d" % i for i in range(N)] + ["arp%d" % i for i in range(N)]
              + ["pm%d" % i for i in range(N)] + ["cp%d" % i for i in range(N)])


def engines(mask):
    return sum((mask >> b) & 1 for b in range(mask.bit_length()))


def plan_of(src, cores, topo):
    others = [c for c in cores if c != src]
    near = [c for c in others if topo.chip(c) == topo.chip(src)]
    far = [c for c in others if topo.chip(c) != topo.chip(src)]
    far.sort(key=lambda c: topo.die(c) != topo.die(src))
    leave = topo.mask(src, far[0])
    whole = topo.mask(src, near[0])
    return near[0], far[0], far[1], leave, whole & ~leave, whole


def rank_program(g, core, T, topo):
    r = T.rank_of(core)
    if r is None:
        return
    S = T.sem
    V, TE, AC, SY = g.vector, g.tensor, g.scalar, g.sync

    def slot(buf, i, w=W):
        return buf[:, w * i:w * i + w]

    def bank(i, w):
        return T.ps[:, BANK * i:BANK * i + w]

    def codes(i):
        return slot(T.t_q, i).bitcast(dt.uint8)

    near, far1, far2, leave, stay, whole = plan_of(core, T.cores, topo)
    jn, j1, j2 = T.rank_of(near), T.rank_of(far1), T.rank_of(far2)
    due = {jn: (engines(stay), engines(stay)), j1: (engines(leave), engines(leave)), j2: (engines(whole), engines(leave))}
    seq = [r, jn, j1, j2]

    Q = 4 * W
    SY.dma_start(T.a_t[:], T.a[:]).then_inc(S.ld_a, 16)
    AC.dma_start(T.xe_t[:, 0:Q], T.x[:]).then_inc(S.ld_x, 16)
    AC.dma_start(T.xe_t[:, Q:2 * Q], T.e[:]).then_inc(S.ld_e, 16)
    SY.dma_start(T.v_t[:], T.v[:]).then_inc(S.ld_v, 16)

    V.wait_ge(S.ld_x, 16)
    V.quantize_mx(slot(T.xe_q, 0), slot(T.xe_s, 0), T.xe_t[:, 0:Q]).then_inc(S.q_x, 1)
    V.wait_ge(S.ld_a, 16)
    for i in range(G):
        V.quantize_mx(slot(T.a_q, i), slot(T.a_s, i), slot(T.a_t, i, Q)).then_inc(S["q_a%d" % i], 1)
    V.wait_ge(S.ld_e, 16)
    V.quantize_mx(slot(T.xe_q, 1), slot(T.xe_s, 1), T.xe_t[:, Q:2 * Q]).then_inc(S.q_e, 1)
    for i in range(G):
        V.wait_ge(S["mu%d" % i], 1)
        V.tensor_scalar(slot(T.mc, i), bank(i, W), 0.0, CONST, AluOpType.is_gt, AluOpType.mult).then_inc(S["ts%d" % i], 1)
    for i in range(G):
        V.wait_ge(S["ts%d" % i], 1)
        V.wait_ge(S["md%d" % i], 1)
        V.tensor_tensor(T.t_t[:, i:Q:4], bank(G + i, W), slot(T.mc, i), AluOpType.mult).then_inc(S["tt%d" % i], 1)
    for i in range(G):
        V.wait_ge(S["tt%d" % i], 1)
    V.quantize_mx(slot(T.t_q, r), slot(T.t_s, r), T.t_t[:]).then_inc(S.q_t, 1)
    V.wait_ge(S.ld_v, 16)
    V.quantize_mx(T.v_q[:], T.v_s[:], T.v_t[:]).then_inc(S.q_v, 1)

    TE.wait_ge(S.q_x, 1)
    for i in range(G):
        TE.wait_ge(S["q_a%d" % i], 1)
        TE.matmul_mx(bank(i, W), slot(T.a_q, i), slot(T.a_s, i),
                     slot(T.xe_q, 0), slot(T.xe_s, 0), True, True).then_inc(S["mu%d" % i], 1)
    TE.wait_ge(S.q_e, 1)
    for i in range(G):
        TE.matmul_mx(bank(G + i, W), slot(T.a_q, i), slot(T.a_s, i),
                     slot(T.xe_q, 1), slot(T.xe_s, 1), True, True).then_inc(S["md%d" % i], 1)

    left = [0]

    def send(ap, sem, where):
        trs = []
        for dst, m in where:
            rid, pid, _ = topo.addr(dst)
            trs.append(RemoteDMATransfer(dst_ids=[DstId(rid=rid, pnc=pid)], dma_engine_mask=m,
                                         remote_sem=sem, src=ap, dst=ap))
            left[0] += engines(m)
        g.remote_dma_fused(trs, local_sem=S.sent)

    g.wait_ge(S.q_t, 1)
    send(codes(r), S["arc%d" % r], [(far1, leave), (near, stay)])
    send(slot(T.t_s, r), S["arp%d" % r], [(far1, leave), (near, stay)])
    send(slot(T.t_s, r), S["arp%d" % r], [(far2, leave)])
    g.wait_ge(S["arc%d" % j1], due[j1][0])
    send(codes(j1), S["arc%d" % j1], [(near, whole)])

    TE.wait_ge(S.q_t, 1)
    TE.wait_ge(S.q_v, 1)
    HV = NV // 2
    for j in seq:
        if j != r:
            TE.wait_ge(S["arc%d" % j], due[j][0])
            TE.wait_ge(S["arp%d" % j], due[j][1])
        if j != seq[-1]:
            TE.matmul_mx(bank(j, NV), slot(T.t_q, j), slot(T.t_s, j),
                         T.v_q[:], T.v_s[:], True, True).then_inc(S["pm%d" % j], 1)
        else:
            TE.matmul_mx(bank(j, HV), slot(T.t_q, j), slot(T.t_s, j),
                         T.v_q[:, 0:HV], T.v_s[:, 0:HV], True, True).then_inc(S["pm%d" % j], 1)
            TE.matmul_mx(bank(N, HV), slot(T.t_q, j), slot(T.t_s, j),
                         T.v_q[:, HV:NV], T.v_s[:, HV:NV], True, True).then_inc(S.pm_b, 1)

    n_sy = n_sc = 0
    for k, j in enumerate(seq):
        src, mid, out = bank(j, NV), slot(T.y_t, j, NV), slot(T.y, j, NV)
        if k == len(seq) - 1:
            V.wait_ge(S["pm%d" % j], 1)
            V.tensor_copy(T.y_t[:, NV * j:NV * j + HV], bank(j, HV)).then_inc(S["cp%d" % j], 1)
            V.wait_ge(S.pm_b, 1)
            V.tensor_copy(T.y_t[:, NV * j + HV:NV * j + NV], bank(N, HV)).then_inc(S.cp_b, 1)
            SY.wait_ge(S["cp%d" % j], 1)
            SY.wait_ge(S.cp_b, 1)
            SY.dma_start(out, mid).then_inc(S.st_sy, 16)
            n_sy += 16
        elif k % 2 == 0:
            AC.wait_ge(S["pm%d" % j], 1)
            AC.activation(mid, src, ActivationFunctionType.Copy).then_inc(S["cp%d" % j], 1)
            AC.wait_ge(S["cp%d" % j], 1)
            AC.dma_start(out, mid).then_inc(S.st_sc, 16)
            n_sc += 16
        else:
            V.wait_ge(S["pm%d" % j], 1)
            V.tensor_copy(mid, src).then_inc(S["cp%d" % j], 1)
            SY.wait_ge(S["cp%d" % j], 1)
            SY.dma_start(out, mid).then_inc(S.st_sy, 16)
            n_sy += 16
    AC.wait_ge(S.st_sc, n_sc)
    SY.wait_ge(S.st_sy, n_sy)
    g.wait_ge(S.sent, left[0])
